import numpy as np
import ml_dtypes


def mxq(x, axis, fmt="e4m3"):
    dtype, down = {"e4m3": (ml_dtypes.float8_e4m3fn, 7), "e5m2": (ml_dtypes.float8_e5m2, 14)}[fmt]
    v = np.moveaxis(np.asarray(x, np.float32).astype(ml_dtypes.bfloat16).astype(np.float64), axis, -1)
    blocks = v.reshape(v.shape[:-1] + (-1, 32))
    amax = np.abs(blocks).max(-1, keepdims=True)
    byte = np.maximum(np.where(amax > 0, np.frexp(amax)[1] - 1 + 127, 0) - down, 1)
    scale = np.exp2(byte - 127.0)
    codes = (blocks / scale).astype(np.float32).astype(dtype).astype(np.float64)
    return np.moveaxis((codes * scale).reshape(v.shape), -1, axis)


WIDE = False


def mx_kscale(k):
    if not WIDE:
        return np.ones(k)
    levels = np.array([10, -10, 5, -5, 0])
    if k % 512:
        return np.exp2(np.random.permutation(np.resize(levels, k // 32))).repeat(32)
    a = np.empty((k // 512, 16))
    for p in range(k // 512):
        a[p, :8] = np.random.permutation(np.resize(levels, 8))
        for g in range(8):
            far = levels[np.abs(levels - a[p, g]) >= 10]
            a[p, g + 8] = far[np.random.randint(len(far))]
    return np.exp2(a.ravel()).repeat(32)


def f64(x):
    return np.asarray(x).astype(np.float64)


def striped(idx):
    return np.tile(idx.reshape(-1, 16).T, (8, 1)).astype(np.uint16)


def unstriped(offs):
    return offs[:16].T.reshape(-1).astype(np.int64)


E2M1 = np.array([0.0, 0.5, 1.0, 1.5, 2.0, 3.0, 4.0, 6.0, -0.0, -0.5, -1.0, -1.5, -2.0, -3.0, -4.0, -6.0])


def pack_weight(w, fmt):
    k, n = w.shape
    w = f64(np.asarray(w, np.float32).astype(ml_dtypes.bfloat16)).reshape(k // 32, 32, n)
    amax = np.abs(w).max(1)
    if fmt == "e4m3":
        byte = np.frexp(amax)[1] - 1 + 127 - 7
    else:
        mant, ex = np.frexp(amax / 6.0)
        byte = np.where(mant > 0.5, ex, ex - 1) + 127
    byte = np.clip(np.where(amax > 0, byte, 1), 1, 254)
    scaled = (w * np.exp2(127.0 - byte)[:, None, :]).reshape(k, n).astype(np.float32)
    by_word = np.ascontiguousarray(scaled.reshape(k // 512, 128, 4, n).transpose(0, 1, 3, 2))
    if fmt == "e4m3":
        words = by_word.astype(ml_dtypes.float8_e4m3fn).view(np.uint8)
    else:
        c = by_word.astype(ml_dtypes.float4_e2m1fn).view(np.uint8) & 0xF
        words = (c[..., 0::2] | (c[..., 1::2] << 4)).reshape(k // 512, 128, 2 * n)
    return np.ascontiguousarray(words), np.ascontiguousarray(byte.astype(np.uint8).reshape(k // 512, 16, n))


def unpack_weight(words, scales, fmt):
    g, _, n = scales.shape
    words = np.ascontiguousarray(words).reshape(g, 128, n, -1)
    if fmt == "e4m3":
        vals = words.view(ml_dtypes.float8_e4m3fn).astype(np.float64)
    else:
        nib = np.empty((g, 128, n, 4), np.uint8)
        nib[..., 0::2] = words & 0xF
        nib[..., 1::2] = words >> 4
        vals = E2M1[nib]
    vals = vals * np.repeat(np.exp2(scales.astype(np.float64) - 127.0), 8, axis=1)[..., None]
    return vals.transpose(0, 1, 3, 2).reshape(g * 512, n)


K, T, E, C, N = 1536, 640, 20, 128, 128
TOP = 4


def by_expert(wq, xq):
    return np.concatenate([wq[e].T @ xq[:, e * C:(e + 1) * C] for e in range(E)], axis=1)


def setup_inputs():
    n = np.random.standard_normal
    s = mx_kscale(K)[:, None]
    deal = np.repeat(np.arange(E), C).reshape(TOP, T)[:, np.random.permutation(T)]
    deal = np.take_along_axis(deal, np.argsort(np.random.rand(TOP, T), axis=0), axis=0)
    for _ in range(8):
        s_, t_ = np.random.permutation(T).reshape(2, -1); r = np.random.randint(TOP, size=T // 2); x, y = deal[r, s_].copy(), deal[r, t_].copy()
        ok = ~((deal[:, s_] == y).any(0) | (deal[:, t_] == x).any(0)); deal[r[ok], s_[ok]] = y[ok]; deal[r[ok], t_[ok]] = x[ok]
    order = np.lexsort((np.random.rand(TOP * T), deal.reshape(-1)))
    slot_token = order % T; pos = np.empty(TOP * T, np.int64); pos[order] = np.arange(TOP * T); pos = pos.reshape(TOP, T)
    g = np.random.uniform(0.5, 1.5, (TOP, T)); g = g / g.sum(0)
    w = [pack_weight(m, "e2m1") for m in n((E + 1, K, N)) / np.sqrt(K) / s[None]]
    return {
        "xT": (n((K, T)) * s).astype(np.float32),
        "w_words": np.stack([m[0] for m in w]),
        "w_scales": np.stack([m[1] for m in w]),
        "b": (0.3 * n((N, E + 1))).astype(np.float32),
        "gate": np.stack([np.tile(r, (N, 1)) for r in g]).astype(np.float32),
        "offs": striped(slot_token),
        "pos1": striped(pos[0]),
        "pos2": striped(pos[1]),
        "pos3": striped(pos[2]),
        "pos4": striped(pos[3]),
    }


def reference(xT, w_words, w_scales, b, gate, offs, pos1, pos2, pos3, pos4):
    idx = unstriped(offs)
    w = np.stack([unpack_weight(w_words[e], w_scales[e], "e2m1") for e in range(E + 1)])
    wq = w
    xs = mxq(f64(xT), 0, "e4m3")
    ys = (wq[E].T @ xs) + f64(b)[:, E:]
    xq = mxq(f64(xT)[:, idx], 0, "e4m3")
    y = by_expert(w, xq)
    y = y + np.repeat(f64(b)[:, :E], C, axis=1)
    return ys + sum(f64(gate[r]) * y[:, unstriped(p)] for r, p in enumerate((pos1, pos2, pos3, pos4)))

@@ -1,0 +1,206 @@
+from contextlib import ExitStack
+
+import concourse.mybir as mybir
+
+K, T, E, C, N = 1536, 640, 20, 128, 128
+TOP = 4
+SLOTS = E * C
+FLOPS = 2 * K * N * (SLOTS + T)
+
+F32 = mybir.dt.float32
+BF16 = mybir.dt.bfloat16
+I32 = mybir.dt.int32
+U32 = mybir.dt.uint32
+U16 = mybir.dt.uint16
+U8 = mybir.dt.uint8
+FP8X4 = mybir.dt.float8_e4m3fn_x4
+FP4X4 = mybir.dt.float4_e2m1fn_x4
+MULT = mybir.AluOpType.mult
+ADD = mybir.AluOpType.add
+IDENTITY = mybir.ActivationFunctionType.Identity
+
+P = 128
+PASSES = 3
+LIST_ROWS = 16
+WINDOW = 1376
+PAD = WINDOW - T
+CHUNKS = [(0, 1024), (1024, 1024), (2048, 512)]
+STEPS = [(0, 0), (0, 1), (0, 2), (1, 0), (2, 0), (1, 1), (2, 1), (1, 2), (2, 2)]
+VECTOR_TOKENS = 448
+BANK = 512
+
+
+def tile_moe_shr_lin_bias_kernel(
+    tc, xT, w_words, w_scales, b, gate, offs, pos1, pos2, pos3, pos4, out
+):
+    nc = tc.nc
+    with ExitStack() as ctx:
+        lists = ctx.enter_context(tc.tile_pool(name="lists", bufs=1))
+        keep = ctx.enter_context(tc.tile_pool(name="keep", bufs=1))
+        ring = ctx.enter_context(tc.tile_pool(name="ring", bufs=3))
+        psum = ctx.enter_context(tc.psum_pool(name="psum", bufs=1))
+
+        pairs = keep.tile([P, 2 * (2 * PASSES * T + PAD)], BF16, align_bytes=64)
+        w_sb = keep.tile([P, (E + 1) * PASSES * 2 * N], U8, align_bytes=64)
+        w_sc = keep.tile([P, (E + 1) * PASSES * N], U8, align_bytes=64)
+        codes = keep.tile([P, PASSES, SLOTS + T], U32, align_bytes=64)
+        scales = keep.tile([P, PASSES, SLOTS + T], U8, align_bytes=64)
+        bias = keep.tile([P, E + 1], F32)
+        gates = keep.tile([P, TOP, T], F32)
+        y = keep.tile([P, SLOTS], F32)
+        ys = keep.tile([P, T], F32)
+        warm = keep.tile([P, 1], F32)
+
+        def plane(a, h):
+            return (2 * (PASSES - 1 - a) + h) * T
+
+        nc.vector.memset(warm[:], 0.0)
+        nc.scalar.activation(warm[:], warm[:], IDENTITY)
+        nc.vector.memset(pairs[:, 2 * 2 * PASSES * T :].bitcast(I32), 0)
+        nc.vector.memset(w_sc[:].bitcast(I32), 0)
+
+        rows = xT.rearrange("(a p h e) t -> a h p e t", a=PASSES, p=P, h=2)
+        raw = {}
+        offs_sb = lists.tile([P, SLOTS // LIST_ROWS], U16)
+        for a in range(PASSES):
+            for h in (1, 0):
+                raw[a, h] = keep.tile([P, 2, T], F32, name="raw%d%d" % (a, h))
+                nc.sync.dma_start(raw[a, h][:], rows[a, h])
+                if (a, h) == (0, 1):
+                    nc.sync.dma_start(offs_sb[:], offs)
+        scale_rows = w_scales.bitcast(I32).rearrange("e a (q r) c -> r q (e a) c", r=4)
+        for r in range(4):
+            nc.sync.dma_start(
+                w_sc[r:P:32, :].bitcast(I32).rearrange("q (m c) -> q m c", c=N // 4), scale_rows[r]
+            )
+        word_rows = w_words.bitcast(I32).rearrange("e a p c -> p (e a) c")
+        w_view = w_sb[:].bitcast(I32).rearrange("p (m c) -> p m c", c=N // 2)
+        for e0, e1 in ((0, 8), (8, 16), (16, E + 1)):
+            nc.sync.dma_start(w_view[:, PASSES * e0 : PASSES * e1, :], word_rows[:, PASSES * e0 : PASSES * e1, :])
+            if e0 == 0:
+                nc.sync.dma_start(bias[:], b)
+        pos_sb = []
+        for r, pos in enumerate((pos1, pos2, pos3, pos4)):
+            pos_sb.append(lists.tile([P, T // LIST_ROWS], U16, name="pos%d" % r))
+            nc.sync.dma_start(pos_sb[r][:], pos)
+        nc.sync.dma_start(gates[:], gate.rearrange("r n t -> n r t"))
+
+        def cast(a, h):
+            dst = pairs[:, 2 * plane(a, h) : 2 * (plane(a, h) + T)].rearrange("p (t e) -> p t e", e=2)
+            src = raw[a, h][:].rearrange("p e t -> p t e")
+            if (a, h) == (0, 1):
+                nc.vector.tensor_copy(dst[:, :VECTOR_TOKENS, :], src[:, :VECTOR_TOKENS, :])
+                nc.scalar.copy(dst[:, VECTOR_TOKENS:, :], src[:, VECTOR_TOKENS:, :])
+            else:
+                nc.scalar.copy(dst, src)
+
+        def gather(a, c):
+            s0, n = CHUNKS[c]
+            halves = ring.tile([P, 2, 2 * n], BF16, name="halves", align_bytes=64)
+            for h in (1, 0):
+                window = pairs[:, 2 * plane(a, h) : 2 * (plane(a, h) + WINDOW)].bitcast(U32)
+                nc.vector.tensor_copy(
+                    halves[:, h, :].bitcast(U32),
+                    window.indirect(offs_sb[:, s0 // LIST_ROWS : (s0 + n) // LIST_ROWS]),
+                )
+            grouped = ring.tile([P, 4 * n], BF16, name="grouped", align_bytes=64)
+            nc.scalar.copy(
+                grouped[:].bitcast(U32).rearrange("p (s h) -> p s h", h=2),
+                halves[:].bitcast(U32).rearrange("p h s -> p s h"),
+            )
+            return grouped
+
+        def quantize(a, s0, n, grouped):
+            nc.vector.quantize_mx(
+                out=codes[:, a, s0 : s0 + n].bitcast(FP8X4), scales=scales[:, a, s0 : s0 + n], in_=grouped
+            )
+
+        def matmul(acc, e, a, s0, n):
+            m = e * PASSES + a
+            nc.tensor.matmul_mx(
+                out=acc,
+                lhsT=w_sb[:, m * 2 * N : (m + 1) * 2 * N].bitcast(FP4X4),
+                lhsT_scale=w_sc[:, m * N : (m + 1) * N],
+                rhs=codes[:, a, s0 : s0 + n].bitcast(FP8X4),
+                rhs_scale=scales[:, a, s0 : s0 + n],
+                start=(a == 0),
+                stop=(a == PASSES - 1),
+            )
+
+        def evacuate(dst, acc, e):
+            nc.scalar.activation(dst, acc, IDENTITY, bias=bias[:, e : e + 1])
+
+        last_first = CHUNKS[-1][0] // C
+        own_bank = {}
+        for e in range(last_first, E):
+            own_bank[e] = psum.tile([P, C], F32, name="own%d" % e)
+
+        def finish(a, c):
+            s0, n = CHUNKS[c]
+            if c == len(CHUNKS) - 1:
+                if a >= 1:
+                    for e in range(last_first, E):
+                        for a2 in (0, 1) if a == 1 else (2,):
+                            matmul(own_bank[e][:], e, a2, e * C, C)
+                        if a == PASSES - 1:
+                            evacuate(y[:, e * C : (e + 1) * C], own_bank[e][:], e)
+            elif a == PASSES - 1:
+                for e0 in range(s0 // C, (s0 + n) // C, 4):
+                    acc = psum.tile([P, BANK], F32, name="acc", bufs=2)
+                    for j in range(4):
+                        for a2 in range(PASSES):
+                            matmul(acc[:, j * C : (j + 1) * C], e0 + j, a2, (e0 + j) * C, C)
+                    for j in range(4):
+                        e = e0 + j
+                        evacuate(y[:, e * C : (e + 1) * C], acc[:, j * C : (j + 1) * C], e)
+
+        shared = {}
+
+        def group_shared(a):
+            shared[a] = keep.tile([P, 4 * T], BF16, name="shared%d" % a, align_bytes=64)
+            nc.scalar.copy(
+                shared[a][:].bitcast(U32).rearrange("p (t h) -> p t h", h=2),
+                pairs[:, 2 * plane(a, 0) : 2 * (plane(a, 0) + 2 * T)].bitcast(U32).rearrange("p (h t) -> p t h", h=2),
+            )
+
+        cast(0, 1)
+        cast(0, 0)
+        pending = None
+        for i, (a, c) in enumerate(STEPS):
+            grouped = gather(a, c)
+            if i < PASSES - 1:
+                cast(i + 1, 1)
+                cast(i + 1, 0)
+            if pending is not None:
+                quantize(pending[0], CHUNKS[pending[1]][0], CHUNKS[pending[1]][1], pending[2][:])
+                finish(pending[0], pending[1])
+            if 2 <= i < 2 + PASSES:
+                group_shared(i - 2)
+            pending = (a, c, grouped)
+        quantize(pending[0], CHUNKS[pending[1]][0], CHUNKS[pending[1]][1], pending[2][:])
+        finish(pending[0], pending[1])
+
+        for t0, n in ((0, BANK), (BANK, T - BANK)):
+            acc = psum.tile([P, n], F32, name="shared_acc%d" % t0)
+            for a in range(PASSES):
+                quantize(a, SLOTS + t0, n, shared[a][:, 4 * t0 : 4 * (t0 + n)])
+                matmul(acc[:], E, a, SLOTS + t0, n)
+            evacuate(ys[:, t0 : t0 + n], acc[:], E)
+
+        terms = [ring.tile([P, T], F32, name="term%d" % r, bufs=1) for r in range(TOP)]
+
+        def fetch(r):
+            nc.vector.tensor_tensor(terms[r][:], y[:].indirect(pos_sb[r][:]), gates[:, r, :], MULT)
+
+        fetch(0)
+        fetch(1)
+        fetch(2)
+        nc.vector.tensor_tensor(ys[:], ys[:], terms[0][:], ADD)
+        fetch(3)
+        nc.vector.tensor_tensor(terms[1][:], terms[1][:], terms[2][:], ADD)
+        cuts = (slice(0, T // 2), slice(T // 2, T))
+        for cols in cuts:
+            nc.vector.tensor_tensor(ys[:, cols], ys[:, cols], terms[3][:, cols], ADD)
+        for cols in cuts:
+            nc.vector.tensor_tensor(ys[:, cols], ys[:, cols], terms[1][:, cols], ADD)
+            nc.sync.dma_start(out[:, cols], ys[:, cols])

@@ -18,16 +18,26 @@ FP4X4 = mybir.dt.float4_e2m1fn_x4
 MULT = mybir.AluOpType.mult
 ADD = mybir.AluOpType.add
 IDENTITY = mybir.ActivationFunctionType.Identity
+COPY = mybir.ActivationFunctionType.Copy
 
 P = 128
 PASSES = 3
 LIST_ROWS = 16
-WINDOW = 1376
-PAD = WINDOW - T
-CHUNKS = [(0, 1024), (1024, 1024), (2048, 512)]
-STEPS = [(0, 0), (0, 1), (0, 2), (1, 0), (2, 0), (1, 1), (2, 1), (1, 2), (2, 2)]
-VECTOR_TOKENS = 448
 BANK = 512
+LOAD_ORDER = [(0, 0), (1, 0), (1, 1), (0, 1), (2, 0), (2, 1)]
+SCALAR_FIRST = 8
+VECTOR_TOKENS = 448
+OWN_FIRST = 16
+
+
+def window_width(n):
+    return 8 * ((4 * n + 23) // 24)
+
+
+PAD = window_width(SLOTS // 2) - T
+END_PAD = window_width(BANK) - T
+PLANE_AT = {(0, 0): 0, (1, 0): T + PAD, (0, 1): 2 * T + PAD, (1, 1): 3 * T + PAD, (2, 0): 4 * T + PAD, (2, 1): 5 * T + PAD}
+WORDS = 6 * T + PAD + END_PAD
 
 
 def tile_moe_shr_lin_bias_kernel(
@@ -37,10 +47,11 @@ def tile_moe_shr_lin_bias_kernel(
     with ExitStack() as ctx:
         lists = ctx.enter_context(tc.tile_pool(name="lists", bufs=1))
         keep = ctx.enter_context(tc.tile_pool(name="keep", bufs=1))
-        ring = ctx.enter_context(tc.tile_pool(name="ring", bufs=3))
+        ring = ctx.enter_context(tc.tile_pool(name="ring", bufs=1))
         psum = ctx.enter_context(tc.psum_pool(name="psum", bufs=1))
 
-        pairs = keep.tile([P, 2 * (2 * PASSES * T + PAD)], BF16, align_bytes=64)
+        pairs = keep.tile([P, 2 * WORDS], BF16, align_bytes=64)
+        singles = keep.tile([P, 2, T], BF16, align_bytes=64)
         w_sb = keep.tile([P, (E + 1) * PASSES * 2 * N], U8, align_bytes=64)
         w_sc = keep.tile([P, (E + 1) * PASSES * N], U8, align_bytes=64)
         codes = keep.tile([P, PASSES, SLOTS + T], U32, align_bytes=64)
@@ -50,70 +61,116 @@ def tile_moe_shr_lin_bias_kernel(
         y = keep.tile([P, SLOTS], F32)
         ys = keep.tile([P, T], F32)
         warm = keep.tile([P, 1], F32)
-
-        def plane(a, h):
-            return (2 * (PASSES - 1 - a) + h) * T
-
-        nc.vector.memset(warm[:], 0.0)
-        nc.scalar.activation(warm[:], warm[:], IDENTITY)
-        nc.vector.memset(pairs[:, 2 * 2 * PASSES * T :].bitcast(I32), 0)
-        nc.vector.memset(w_sc[:].bitcast(I32), 0)
-
-        rows = xT.rearrange("(a p h e) t -> a h p e t", a=PASSES, p=P, h=2)
-        raw = {}
+        early = [keep.tile([P, 2, 2 * SLOTS], BF16, name="early%d" % a, align_bytes=64) for a in range(2)]
         offs_sb = lists.tile([P, SLOTS // LIST_ROWS], U16)
-        for a in range(PASSES):
-            for h in (1, 0):
-                raw[a, h] = keep.tile([P, 2, T], F32, name="raw%d%d" % (a, h))
+        pos_sb = [lists.tile([P, T // LIST_ROWS], U16, name="pos%d" % r) for r in range(TOP)]
+
+        nc.gpsimd.memset(warm[:], 0.0)
+        nc.scalar.activation(warm[:], warm[:], IDENTITY)
+        nc.gpsimd.memset(pairs[:, 2 * T : 2 * (T + PAD)].bitcast(I32), 0)
+        nc.gpsimd.memset(pairs[:, 2 * (WORDS - END_PAD) :].bitcast(I32), 0)
+        nc.gpsimd.memset(w_sc[:].bitcast(I32), 0)
+
+        def slot_offsets(s0, n):
+            return offs_sb[:, s0 // LIST_ROWS : (s0 + n) // LIST_ROWS]
+
+        def gather_pairs(dst, a, h, s0, n):
+            first = PLANE_AT[a, h]
+            window = pairs[:, 2 * first : 2 * (first + window_width(n))].bitcast(U32)
+            nc.vector.tensor_copy(dst.bitcast(U32), window.indirect(slot_offsets(s0, n)))
+
+        def gather_early(a, h, s0, n):
+            gather_pairs(early[a][:, h, 2 * s0 : 2 * (s0 + n)], a, h, s0, n)
+
+        def gather_singles(e0, e1):
+            for j in range(2):
+                for e in range(e0, e1):
+                    dst = early[1][:, 1, 2 * e * C : 2 * (e + 1) * C].rearrange("p (s j) -> p j s", j=2)
+                    nc.scalar.activation(dst[:, j, :], singles[:, j, :].indirect(slot_offsets(e * C, C)), COPY)
+
+        with tc.tile_pool(name="raw", bufs=1) as raw_pool:
+            rows = xT.rearrange("(a p h j) t -> a h p j t", a=PASSES, p=P, h=2)
+            scale_rows = w_scales.bitcast(I32).rearrange("e a (q r) c -> r q (e a) c", r=4)
+            word_rows = w_words.bitcast(I32).rearrange("e a p c -> p (e a) c")
+            w_view = w_sb[:].bitcast(I32).rearrange("p (m c) -> p m c", c=N // 2)
+            raw = {}
+
+            def load_tokens(a, h):
+                raw[a, h] = raw_pool.tile([P, 2, T], F32, name="raw%d%d" % (a, h))
                 nc.sync.dma_start(raw[a, h][:], rows[a, h])
-                if (a, h) == (0, 1):
-                    nc.sync.dma_start(offs_sb[:], offs)
-        scale_rows = w_scales.bitcast(I32).rearrange("e a (q r) c -> r q (e a) c", r=4)
-        for r in range(4):
-            nc.sync.dma_start(
-                w_sc[r:P:32, :].bitcast(I32).rearrange("q (m c) -> q m c", c=N // 4), scale_rows[r]
-            )
-        word_rows = w_words.bitcast(I32).rearrange("e a p c -> p (e a) c")
-        w_view = w_sb[:].bitcast(I32).rearrange("p (m c) -> p m c", c=N // 2)
-        for e0, e1 in ((0, 8), (8, 16), (16, E + 1)):
-            nc.sync.dma_start(w_view[:, PASSES * e0 : PASSES * e1, :], word_rows[:, PASSES * e0 : PASSES * e1, :])
-            if e0 == 0:
-                nc.sync.dma_start(bias[:], b)
-        pos_sb = []
-        for r, pos in enumerate((pos1, pos2, pos3, pos4)):
-            pos_sb.append(lists.tile([P, T // LIST_ROWS], U16, name="pos%d" % r))
-            nc.sync.dma_start(pos_sb[r][:], pos)
-        nc.sync.dma_start(gates[:], gate.rearrange("r n t -> n r t"))
 
-        def cast(a, h):
-            dst = pairs[:, 2 * plane(a, h) : 2 * (plane(a, h) + T)].rearrange("p (t e) -> p t e", e=2)
-            src = raw[a, h][:].rearrange("p e t -> p t e")
-            if (a, h) == (0, 1):
-                nc.vector.tensor_copy(dst[:, :VECTOR_TOKENS, :], src[:, :VECTOR_TOKENS, :])
-                nc.scalar.copy(dst[:, VECTOR_TOKENS:, :], src[:, VECTOR_TOKENS:, :])
+            def load_scales(e0, e1):
+                mats = slice(PASSES * e0, PASSES * e1)
+                for r in range(4):
+                    live = w_sc[r:P:32, :].bitcast(I32).rearrange("q (m c) -> q m c", c=N // 4)
+                    nc.sync.dma_start(live[:, mats, :], scale_rows[r][:, mats, :])
+
+            def load_words(e0, e1):
+                mats = slice(PASSES * e0, PASSES * e1)
+                nc.sync.dma_start(w_view[:, mats, :], word_rows[:, mats, :])
+
+            load_tokens(0, 0)
+            nc.sync.dma_start(offs_sb[:], offs)
+            for a, h in LOAD_ORDER[1:]:
+                load_tokens(a, h)
+            load_scales(0, 8)
+            load_words(0, 8)
+            nc.sync.dma_start(bias[:], b)
+            load_scales(8, E + 1)
+            load_words(8, 16)
+            load_words(16, E + 1)
+            for r, pos in enumerate((pos1, pos2, pos3, pos4)):
+                nc.sync.dma_start(pos_sb[r][:], pos)
+            nc.sync.dma_start(gates[:], gate.rearrange("r n t -> n r t"))
+
+            def cast(a, h):
+                first = PLANE_AT[a, h]
+                dst = pairs[:, 2 * first : 2 * (first + T)].rearrange("p (t j) -> p t j", j=2)
+                src = raw[a, h][:].rearrange("p j t -> p t j")
+                if (a, h) == LOAD_ORDER[0]:
+                    nc.vector.tensor_copy(dst[:, :VECTOR_TOKENS, :], src[:, :VECTOR_TOKENS, :])
+                    nc.scalar.copy(dst[:, VECTOR_TOKENS:, :], src[:, VECTOR_TOKENS:, :])
+                else:
+                    nc.scalar.copy(dst, src)
+
+            cast(0, 0)
+            gather_early(0, 0, 0, SLOTS // 2)
+            gather_early(0, 0, SLOTS // 2, SLOTS // 2)
+            cast(1, 0)
+            cast(1, 1)
+            cast(0, 1)
+            nc.scalar.copy(singles[:], raw[1, 1][:])
+            cast(2, 0)
+            cast(2, 1)
+
+        late = ctx.enter_context(tc.tile_pool(name="late", bufs=1))
+        last_halves = {}
+        grouped = {}
+        shared = {}
+        accs = {}
+
+        def gather_last(c):
+            last_halves[c] = ring.tile([P, 2, 2 * BANK], BF16, name="last_halves", align_bytes=64, bufs=2)
+            for h in range(2):
+                gather_pairs(last_halves[c][:, h, :], PASSES - 1, h, c * BANK, BANK)
+
+        def interleave(a, s0, n):
+            if a == PASSES - 1:
+                src = last_halves[s0 // BANK][:].bitcast(U32)
             else:
-                nc.scalar.copy(dst, src)
-
-        def gather(a, c):
-            s0, n = CHUNKS[c]
-            halves = ring.tile([P, 2, 2 * n], BF16, name="halves", align_bytes=64)
-            for h in (1, 0):
-                window = pairs[:, 2 * plane(a, h) : 2 * (plane(a, h) + WINDOW)].bitcast(U32)
-                nc.vector.tensor_copy(
-                    halves[:, h, :].bitcast(U32),
-                    window.indirect(offs_sb[:, s0 // LIST_ROWS : (s0 + n) // LIST_ROWS]),
-                )
-            grouped = ring.tile([P, 4 * n], BF16, name="grouped", align_bytes=64)
+                src = early[a][:].bitcast(U32)[:, :, s0 : s0 + n]
+            grouped[a, s0] = ring.tile([P, 4 * n], BF16, name="grouped", align_bytes=64, bufs=3)
             nc.scalar.copy(
-                grouped[:].bitcast(U32).rearrange("p (s h) -> p s h", h=2),
-                halves[:].bitcast(U32).rearrange("p h s -> p s h"),
+                grouped[a, s0][:].bitcast(U32).rearrange("p (s h) -> p s h", h=2), src.rearrange("p h s -> p s h")
             )
-            return grouped
 
-        def quantize(a, s0, n, grouped):
+        def quantize_from(src, a, s0, n):
             nc.vector.quantize_mx(
-                out=codes[:, a, s0 : s0 + n].bitcast(FP8X4), scales=scales[:, a, s0 : s0 + n], in_=grouped
+                out=codes[:, a, s0 : s0 + n].bitcast(FP8X4), scales=scales[:, a, s0 : s0 + n], in_=src
             )
+
+        def quantize(a, s0, n):
+            quantize_from(grouped[a, s0][:], a, s0, n)
 
         def matmul(acc, e, a, s0, n):
             m = e * PASSES + a
@@ -127,67 +184,95 @@ def tile_moe_shr_lin_bias_kernel(
                 stop=(a == PASSES - 1),
             )
 
-        def evacuate(dst, acc, e):
-            nc.scalar.activation(dst, acc, IDENTITY, bias=bias[:, e : e + 1])
+        def open_own():
+            for e in range(OWN_FIRST, E):
+                own = psum.tile([P, C], F32, name="own%d" % e)
+                accs[e] = own[:]
+                for a in range(PASSES - 1):
+                    matmul(accs[e], e, a, e * C, C)
 
-        last_first = CHUNKS[-1][0] // C
-        own_bank = {}
-        for e in range(last_first, E):
-            own_bank[e] = psum.tile([P, C], F32, name="own%d" % e)
-
-        def finish(a, c):
-            s0, n = CHUNKS[c]
-            if c == len(CHUNKS) - 1:
-                if a >= 1:
-                    for e in range(last_first, E):
-                        for a2 in (0, 1) if a == 1 else (2,):
-                            matmul(own_bank[e][:], e, a2, e * C, C)
-                        if a == PASSES - 1:
-                            evacuate(y[:, e * C : (e + 1) * C], own_bank[e][:], e)
-            elif a == PASSES - 1:
-                for e0 in range(s0 // C, (s0 + n) // C, 4):
-                    acc = psum.tile([P, BANK], F32, name="acc", bufs=2)
-                    for j in range(4):
-                        for a2 in range(PASSES):
-                            matmul(acc[:, j * C : (j + 1) * C], e0 + j, a2, (e0 + j) * C, C)
-                    for j in range(4):
-                        e = e0 + j
-                        evacuate(y[:, e * C : (e + 1) * C], acc[:, j * C : (j + 1) * C], e)
-
-        shared = {}
+        def experts(c):
+            if 4 * c >= OWN_FIRST:
+                for e in range(4 * c, 4 * c + 4):
+                    matmul(accs[e], e, PASSES - 1, e * C, C)
+            else:
+                acc = psum.tile([P, BANK], F32, name="acc", bufs=2)
+                for j in range(4):
+                    e = 4 * c + j
+                    accs[e] = acc[:, j * C : (j + 1) * C]
+                    for a in range(PASSES):
+                        matmul(accs[e], e, a, e * C, C)
+            for e in range(4 * c, 4 * c + 4):
+                nc.scalar.activation(y[:, e * C : (e + 1) * C], accs[e], IDENTITY, bias=bias[:, e : e + 1])
 
         def group_shared(a):
-            shared[a] = keep.tile([P, 4 * T], BF16, name="shared%d" % a, align_bytes=64)
+            lo, hi = PLANE_AT[a, 0], PLANE_AT[a, 1]
+            shared[a] = late.tile([P, 4 * T], BF16, name="shared%d" % a, align_bytes=64)
             nc.scalar.copy(
                 shared[a][:].bitcast(U32).rearrange("p (t h) -> p t h", h=2),
-                pairs[:, 2 * plane(a, 0) : 2 * (plane(a, 0) + 2 * T)].bitcast(U32).rearrange("p (h t) -> p t h", h=2),
+                pairs[:, 2 * lo : 2 * (2 * hi - lo)].bitcast(U32).rearrange("p (h t) -> p t h", h=2)[:, :T, :],
             )
 
-        cast(0, 1)
-        cast(0, 0)
-        pending = None
-        for i, (a, c) in enumerate(STEPS):
-            grouped = gather(a, c)
-            if i < PASSES - 1:
-                cast(i + 1, 1)
-                cast(i + 1, 0)
-            if pending is not None:
-                quantize(pending[0], CHUNKS[pending[1]][0], CHUNKS[pending[1]][1], pending[2][:])
-                finish(pending[0], pending[1])
-            if 2 <= i < 2 + PASSES:
-                group_shared(i - 2)
-            pending = (a, c, grouped)
-        quantize(pending[0], CHUNKS[pending[1]][0], CHUNKS[pending[1]][1], pending[2][:])
-        finish(pending[0], pending[1])
+        token_cuts = ((0, BANK), (BANK, T - BANK))
 
-        for t0, n in ((0, BANK), (BANK, T - BANK)):
+        def quantize_shared(a):
+            for t0, n in token_cuts:
+                quantize_from(shared[a][:, 4 * t0 : 4 * (t0 + n)], a, SLOTS + t0, n)
+
+        gather_early(1, 0, 0, SLOTS // 2)
+        gather_early(1, 0, SLOTS // 2, SLOTS // 2)
+        gather_early(0, 1, 0, 1024)
+        gather_early(0, 1, 1024, 1536)
+        gather_early(1, 1, 0, SCALAR_FIRST * C)
+        gather_singles(SCALAR_FIRST, 15)
+        interleave(0, 0, 1024)
+        gather_singles(15, 18)
+        interleave(0, 1024, 1024)
+        gather_singles(18, E)
+        interleave(1, 0, 1024)
+        gather_last(0)
+        gather_last(1)
+        quantize(0, 0, 1024)
+        quantize(0, 1024, 1024)
+        quantize(1, 0, 1024)
+        group_shared(0)
+        interleave(2, 0, BANK)
+        interleave(0, 2048, BANK)
+        quantize(0, 2048, BANK)
+        quantize(2, 0, BANK)
+        gather_last(2)
+        interleave(1, 1024, 1024)
+        interleave(2, 512, BANK)
+        quantize(1, 1024, 1024)
+        quantize(2, 512, BANK)
+        experts(0)
+        gather_last(3)
+        interleave(2, 1024, BANK)
+        interleave(1, 2048, BANK)
+        quantize(2, 1024, BANK)
+        quantize(1, 2048, BANK)
+        experts(1)
+        open_own()
+        gather_last(4)
+        interleave(2, 1536, BANK)
+        group_shared(1)
+        quantize(2, 1536, BANK)
+        experts(2)
+        interleave(2, 2048, BANK)
+        group_shared(2)
+        quantize_shared(0)
+        quantize_shared(1)
+        quantize(2, 2048, BANK)
+        experts(3)
+        experts(4)
+        quantize_shared(2)
+        for t0, n in token_cuts:
             acc = psum.tile([P, n], F32, name="shared_acc%d" % t0)
             for a in range(PASSES):
-                quantize(a, SLOTS + t0, n, shared[a][:, 4 * t0 : 4 * (t0 + n)])
                 matmul(acc[:], E, a, SLOTS + t0, n)
-            evacuate(ys[:, t0 : t0 + n], acc[:], E)
+            nc.scalar.activation(ys[:, t0 : t0 + n], acc[:], IDENTITY, bias=bias[:, E : E + 1])
 
-        terms = [ring.tile([P, T], F32, name="term%d" % r, bufs=1) for r in range(TOP)]
+        terms = [late.tile([P, T], F32, name="term%d" % r) for r in range(TOP)]
 
         def fetch(r):
             nc.vector.tensor_tensor(terms[r][:], y[:].indirect(pos_sb[r][:]), gates[:, r, :], MULT)

@@ -25,19 +25,20 @@ PASSES = 3
 LIST_ROWS = 16
 BANK = 512
 LOAD_ORDER = [(0, 0), (1, 0), (1, 1), (0, 1), (2, 0), (2, 1)]
-SCALAR_FIRST = 8
+SCALAR_FIRST = 0
 VECTOR_TOKENS = 448
 OWN_FIRST = 16
+SHARED_AT = [7 * C, 11 * C, 7 * C]
+VECTOR_EXPERTS = 2
 
 
 def window_width(n):
-    return 8 * ((4 * n + 23) // 24)
+    return max(T, 8 * ((4 * n + 23) // 24))
 
 
-PAD = window_width(SLOTS // 2) - T
-END_PAD = window_width(BANK) - T
-PLANE_AT = {(0, 0): 0, (1, 0): T + PAD, (0, 1): 2 * T + PAD, (1, 1): 3 * T + PAD, (2, 0): 4 * T + PAD, (2, 1): 5 * T + PAD}
-WORDS = 6 * T + PAD + END_PAD
+PLANE_SLOT = {(1, 0): 0, (0, 0): 1, (0, 1): 4, (1, 1): 5, (2, 0): 6, (2, 1): 7}
+PLANE_SLOTS = 8
+WORDS = (PLANE_SLOTS - 1) * T + window_width(BANK)
 
 
 def tile_moe_shr_lin_bias_kernel(
@@ -54,8 +55,8 @@ def tile_moe_shr_lin_bias_kernel(
         singles = keep.tile([P, 2, T], BF16, align_bytes=64)
         w_sb = keep.tile([P, (E + 1) * PASSES * 2 * N], U8, align_bytes=64)
         w_sc = keep.tile([P, (E + 1) * PASSES * N], U8, align_bytes=64)
-        codes = keep.tile([P, PASSES, SLOTS + T], U32, align_bytes=64)
-        scales = keep.tile([P, PASSES, SLOTS + T], U8, align_bytes=64)
+        codes = keep.tile([P, PASSES, SLOTS], U32, align_bytes=64)
+        scales = keep.tile([P, PASSES, SLOTS], U8, align_bytes=64)
         bias = keep.tile([P, E + 1], F32)
         gates = keep.tile([P, TOP, T], F32)
         y = keep.tile([P, SLOTS], F32)
@@ -67,15 +68,15 @@ def tile_moe_shr_lin_bias_kernel(
 
         nc.gpsimd.memset(warm[:], 0.0)
         nc.scalar.activation(warm[:], warm[:], IDENTITY)
-        nc.gpsimd.memset(pairs[:, 2 * T : 2 * (T + PAD)].bitcast(I32), 0)
-        nc.gpsimd.memset(pairs[:, 2 * (WORDS - END_PAD) :].bitcast(I32), 0)
+        nc.vector.memset(pairs[:, 2 * 2 * T : 2 * (T + window_width(SLOTS // 2))].bitcast(I32), 0)
+        nc.vector.memset(pairs[:, 2 * PLANE_SLOTS * T :].bitcast(I32), 0)
         nc.gpsimd.memset(w_sc[:].bitcast(I32), 0)
 
         def slot_offsets(s0, n):
             return offs_sb[:, s0 // LIST_ROWS : (s0 + n) // LIST_ROWS]
 
         def gather_pairs(dst, a, h, s0, n):
-            first = PLANE_AT[a, h]
+            first = PLANE_SLOT[a, h] * T
             window = pairs[:, 2 * first : 2 * (first + window_width(n))].bitcast(U32)
             nc.vector.tensor_copy(dst.bitcast(U32), window.indirect(slot_offsets(s0, n)))
 
@@ -116,30 +117,33 @@ def tile_moe_shr_lin_bias_kernel(
             load_scales(0, 8)
             load_words(0, 8)
             nc.sync.dma_start(bias[:], b)
-            load_scales(8, E + 1)
+            load_scales(8, 16)
             load_words(8, 16)
+            load_scales(16, E + 1)
             load_words(16, E + 1)
             for r, pos in enumerate((pos1, pos2, pos3, pos4)):
                 nc.sync.dma_start(pos_sb[r][:], pos)
             nc.sync.dma_start(gates[:], gate.rearrange("r n t -> n r t"))
 
             def cast(a, h):
-                first = PLANE_AT[a, h]
+                first = PLANE_SLOT[a, h] * T
                 dst = pairs[:, 2 * first : 2 * (first + T)].rearrange("p (t j) -> p t j", j=2)
                 src = raw[a, h][:].rearrange("p j t -> p t j")
                 if (a, h) == LOAD_ORDER[0]:
                     nc.vector.tensor_copy(dst[:, :VECTOR_TOKENS, :], src[:, :VECTOR_TOKENS, :])
                     nc.scalar.copy(dst[:, VECTOR_TOKENS:, :], src[:, VECTOR_TOKENS:, :])
-                else:
+                elif (a, h) == LOAD_ORDER[1]:
                     nc.scalar.copy(dst, src)
+                else:
+                    nc.gpsimd.tensor_scalar(dst, src, 1.0, 0.0, MULT, ADD)
 
             cast(0, 0)
             gather_early(0, 0, 0, SLOTS // 2)
             gather_early(0, 0, SLOTS // 2, SLOTS // 2)
             cast(1, 0)
+            nc.scalar.copy(singles[:], raw[1, 1][:])
             cast(1, 1)
             cast(0, 1)
-            nc.scalar.copy(singles[:], raw[1, 1][:])
             cast(2, 0)
             cast(2, 1)
 
@@ -191,7 +195,7 @@ def tile_moe_shr_lin_bias_kernel(
                 for a in range(PASSES - 1):
                     matmul(accs[e], e, a, e * C, C)
 
-        def experts(c):
+        def multiply(c):
             if 4 * c >= OWN_FIRST:
                 for e in range(4 * c, 4 * c + 4):
                     matmul(accs[e], e, PASSES - 1, e * C, C)
@@ -202,74 +206,90 @@ def tile_moe_shr_lin_bias_kernel(
                     accs[e] = acc[:, j * C : (j + 1) * C]
                     for a in range(PASSES):
                         matmul(accs[e], e, a, e * C, C)
+
+        def evacuate(c):
             for e in range(4 * c, 4 * c + 4):
-                nc.scalar.activation(y[:, e * C : (e + 1) * C], accs[e], IDENTITY, bias=bias[:, e : e + 1])
+                if e >= E - VECTOR_EXPERTS:
+                    nc.vector.tensor_scalar_add(y[:, e * C : (e + 1) * C], accs[e], bias[:, e : e + 1])
+                else:
+                    nc.scalar.activation(y[:, e * C : (e + 1) * C], accs[e], IDENTITY, bias=bias[:, e : e + 1])
+
+        planes = pairs[:, : 2 * PLANE_SLOTS * T].rearrange("p (g t j) -> p g t j", t=T, j=2)
 
         def group_shared(a):
-            lo, hi = PLANE_AT[a, 0], PLANE_AT[a, 1]
+            lo, hi = PLANE_SLOT[a, 0], PLANE_SLOT[a, 1]
             shared[a] = late.tile([P, 4 * T], BF16, name="shared%d" % a, align_bytes=64)
-            nc.scalar.copy(
-                shared[a][:].bitcast(U32).rearrange("p (t h) -> p t h", h=2),
-                pairs[:, 2 * lo : 2 * (2 * hi - lo)].bitcast(U32).rearrange("p (h t) -> p t h", h=2)[:, :T, :],
+            nc.gpsimd.tensor_scalar(
+                shared[a][:].rearrange("p (t h j) -> p t h j", h=2, j=2),
+                planes[:, lo : hi + 1 : hi - lo, :, :].rearrange("p h t j -> p t h j"),
+                1.0,
+                0.0,
+                MULT,
+                ADD,
             )
 
         token_cuts = ((0, BANK), (BANK, T - BANK))
 
         def quantize_shared(a):
             for t0, n in token_cuts:
-                quantize_from(shared[a][:, 4 * t0 : 4 * (t0 + n)], a, SLOTS + t0, n)
+                quantize_from(shared[a][:, 4 * t0 : 4 * (t0 + n)], a, SHARED_AT[a] + t0, n)
 
+        group_shared(0)
+        group_shared(1)
+        group_shared(2)
         gather_early(1, 0, 0, SLOTS // 2)
         gather_early(1, 0, SLOTS // 2, SLOTS // 2)
         gather_early(0, 1, 0, 1024)
         gather_early(0, 1, 1024, 1536)
-        gather_early(1, 1, 0, SCALAR_FIRST * C)
-        gather_singles(SCALAR_FIRST, 15)
+        gather_singles(0, 14)
         interleave(0, 0, 1024)
-        gather_singles(15, 18)
+        gather_singles(14, 16)
         interleave(0, 1024, 1024)
-        gather_singles(18, E)
+        gather_singles(16, 18)
         interleave(1, 0, 1024)
         gather_last(0)
+        interleave(2, 0, BANK)
         gather_last(1)
+        gather_singles(18, E)
         quantize(0, 0, 1024)
         quantize(0, 1024, 1024)
-        quantize(1, 0, 1024)
-        group_shared(0)
-        interleave(2, 0, BANK)
         interleave(0, 2048, BANK)
         quantize(0, 2048, BANK)
-        quantize(2, 0, BANK)
         gather_last(2)
-        interleave(1, 1024, 1024)
+        quantize(2, 0, BANK)
         interleave(2, 512, BANK)
+        quantize(1, 0, 1024)
+        interleave(1, 1024, 1024)
         quantize(1, 1024, 1024)
+        multiply(0)
+        evacuate(0)
         quantize(2, 512, BANK)
-        experts(0)
         gather_last(3)
         interleave(2, 1024, BANK)
         interleave(1, 2048, BANK)
         quantize(2, 1024, BANK)
         quantize(1, 2048, BANK)
-        experts(1)
-        open_own()
         gather_last(4)
+        multiply(1)
+        open_own()
         interleave(2, 1536, BANK)
-        group_shared(1)
         quantize(2, 1536, BANK)
-        experts(2)
         interleave(2, 2048, BANK)
-        group_shared(2)
+        evacuate(1)
+        multiply(2)
         quantize_shared(0)
-        quantize_shared(1)
+        evacuate(2)
         quantize(2, 2048, BANK)
-        experts(3)
-        experts(4)
+        multiply(3)
+        evacuate(3)
+        quantize_shared(1)
         quantize_shared(2)
+        multiply(4)
+        evacuate(4)
         for t0, n in token_cuts:
             acc = psum.tile([P, n], F32, name="shared_acc%d" % t0)
             for a in range(PASSES):
-                matmul(acc[:], E, a, SLOTS + t0, n)
+                matmul(acc[:], E, a, SHARED_AT[a] + t0, n)
             nc.scalar.activation(ys[:, t0 : t0 + n], acc[:], IDENTITY, bias=bias[:, E : E + 1])
 
         terms = [late.tile([P, T], F32, name="term%d" % r) for r in range(TOP)]

@@ -1,6 +1,7 @@
 from contextlib import ExitStack
 
 import concourse.mybir as mybir
+from concourse.masks import make_identity
 
 K, T, E, C, N = 1536, 640, 20, 128, 128
 TOP = 4
@@ -62,6 +63,7 @@ def tile_moe_shr_lin_bias_kernel(
         y = keep.tile([P, SLOTS], F32)
         ys = keep.tile([P, T], F32)
         warm = keep.tile([P, 1], F32)
+        ident = keep.tile([P, P], F32)
         early = [keep.tile([P, 2, 2 * SLOTS], BF16, name="early%d" % a, align_bytes=64) for a in range(2)]
         offs_sb = lists.tile([P, SLOTS // LIST_ROWS], U16)
         pos_sb = [lists.tile([P, T // LIST_ROWS], U16, name="pos%d" % r) for r in range(TOP)]
@@ -70,7 +72,8 @@ def tile_moe_shr_lin_bias_kernel(
         nc.scalar.activation(warm[:], warm[:], IDENTITY)
         nc.vector.memset(pairs[:, 2 * 2 * T : 2 * (T + window_width(SLOTS // 2))].bitcast(I32), 0)
         nc.vector.memset(pairs[:, 2 * PLANE_SLOTS * T :].bitcast(I32), 0)
-        nc.gpsimd.memset(w_sc[:].bitcast(I32), 0)
+        nc.vector.memset(w_sc[:].bitcast(I32), 0)
+        make_identity(nc, ident[:])
 
         def slot_offsets(s0, n):
             return offs_sb[:, s0 // LIST_ROWS : (s0 + n) // LIST_ROWS]
@@ -297,15 +300,33 @@ def tile_moe_shr_lin_bias_kernel(
         def fetch(r):
             nc.vector.tensor_tensor(terms[r][:], y[:].indirect(pos_sb[r][:]), gates[:, r, :], MULT)
 
+        blocks = T // P
+        turned = [psum.tile([P, P], F32, name="own%d" % (OWN_FIRST + i)) for i in range(blocks - 1)]
+        turned.append(psum.tile([P, P], F32, name="acc", bufs=2))
+
+        def add_turned(src, start, stop):
+            for i in range(blocks):
+                nc.tensor.matmul(
+                    turned[i][:], src[:, i * P : (i + 1) * P], ident[:], start=start, stop=stop, is_transpose=True
+                )
+
+        add_turned(ys, True, False)
         fetch(0)
+        add_turned(terms[0], False, False)
         fetch(1)
+        add_turned(terms[1], False, True)
         fetch(2)
-        nc.vector.tensor_tensor(ys[:], ys[:], terms[0][:], ADD)
         fetch(3)
-        nc.vector.tensor_tensor(terms[1][:], terms[1][:], terms[2][:], ADD)
-        cuts = (slice(0, T // 2), slice(T // 2, T))
+        partial = late.tile([P, blocks, P], F32)
+        split = 3 * P
+        back = [psum.tile([P, split], F32, name="acc", bufs=2), psum.tile([P, T - split], F32, name="shared_acc0")]
+        for i in range(blocks):
+            nc.scalar.copy(partial[:, i, :], turned[i][:])
+            col = i * P % split
+            nc.tensor.transpose(back[i * P // split][:, col : col + P], partial[:, i, :], ident[:])
+        cuts = (slice(0, split), slice(split, T))
+        for half, cols in enumerate(cuts):
+            nc.vector.tensor_tensor(terms[2][:, cols], back[half][:], terms[2][:, cols], ADD)
         for cols in cuts:
-            nc.vector.tensor_tensor(ys[:, cols], ys[:, cols], terms[3][:, cols], ADD)
-        for cols in cuts:
-            nc.vector.tensor_tensor(ys[:, cols], ys[:, cols], terms[1][:, cols], ADD)
-            nc.sync.dma_start(out[:, cols], ys[:, cols])
+            nc.vector.tensor_tensor(terms[2][:, cols], terms[2][:, cols], terms[3][:, cols], ADD)
+            nc.sync.dma_start(out[:, cols], terms[2][:, cols])

from contextlib import ExitStack

import concourse.mybir as mybir
from concourse.masks import make_identity

K, T, E, C, N = 1536, 640, 20, 128, 128
TOP = 4
SLOTS = E * C
FLOPS = 2 * K * N * (SLOTS + T)

F32 = mybir.dt.float32
BF16 = mybir.dt.bfloat16
I32 = mybir.dt.int32
U32 = mybir.dt.uint32
U16 = mybir.dt.uint16
U8 = mybir.dt.uint8
FP8X4 = mybir.dt.float8_e4m3fn_x4
FP4X4 = mybir.dt.float4_e2m1fn_x4
MULT = mybir.AluOpType.mult
ADD = mybir.AluOpType.add
IDENTITY = mybir.ActivationFunctionType.Identity
COPY = mybir.ActivationFunctionType.Copy

P = 128
PASSES = 3
LIST_ROWS = 16
BANK = 512
LOAD_ORDER = [(0, 0), (1, 0), (1, 1), (0, 1), (2, 0), (2, 1)]
SCALAR_FIRST = 0
VECTOR_TOKENS = 448
OWN_FIRST = 16
SHARED_AT = [7 * C, 11 * C, 7 * C]
VECTOR_EXPERTS = 2


def window_width(n):
    return max(T, 8 * ((4 * n + 23) // 24))


PLANE_SLOT = {(1, 0): 0, (0, 0): 1, (0, 1): 4, (1, 1): 5, (2, 0): 6, (2, 1): 7}
PLANE_SLOTS = 8
WORDS = (PLANE_SLOTS - 1) * T + window_width(BANK)


def tile_moe_shr_lin_bias_kernel(
    tc, xT, w_words, w_scales, b, gate, offs, pos1, pos2, pos3, pos4, out
):
    nc = tc.nc
    with ExitStack() as ctx:
        lists = ctx.enter_context(tc.tile_pool(name="lists", bufs=1))
        keep = ctx.enter_context(tc.tile_pool(name="keep", bufs=1))
        ring = ctx.enter_context(tc.tile_pool(name="ring", bufs=1))
        psum = ctx.enter_context(tc.psum_pool(name="psum", bufs=1))

        pairs = keep.tile([P, 2 * WORDS], BF16, align_bytes=64)
        singles = keep.tile([P, 2, T], BF16, align_bytes=64)
        w_sb = keep.tile([P, (E + 1) * PASSES * 2 * N], U8, align_bytes=64)
        w_sc = keep.tile([P, (E + 1) * PASSES * N], U8, align_bytes=64)
        codes = keep.tile([P, PASSES, SLOTS], U32, align_bytes=64)
        scales = keep.tile([P, PASSES, SLOTS], U8, align_bytes=64)
        bias = keep.tile([P, E + 1], F32)
        gates = keep.tile([P, TOP, T], F32)
        y = keep.tile([P, SLOTS], F32)
        ys = keep.tile([P, T], F32)
        warm = keep.tile([P, 1], F32)
        ident = keep.tile([P, P], F32)
        early = [keep.tile([P, 2, 2 * SLOTS], BF16, name="early%d" % a, align_bytes=64) for a in range(2)]
        offs_sb = lists.tile([P, SLOTS // LIST_ROWS], U16)
        pos_sb = [lists.tile([P, T // LIST_ROWS], U16, name="pos%d" % r) for r in range(TOP)]

        nc.gpsimd.memset(warm[:], 0.0)
        nc.scalar.activation(warm[:], warm[:], IDENTITY)
        nc.vector.memset(pairs[:, 2 * 2 * T : 2 * (T + window_width(SLOTS // 2))].bitcast(I32), 0)
        nc.vector.memset(pairs[:, 2 * PLANE_SLOTS * T :].bitcast(I32), 0)
        nc.vector.memset(w_sc[:].bitcast(I32), 0)
        make_identity(nc, ident[:])

        def slot_offsets(s0, n):
            return offs_sb[:, s0 // LIST_ROWS : (s0 + n) // LIST_ROWS]

        def gather_pairs(dst, a, h, s0, n):
            first = PLANE_SLOT[a, h] * T
            window = pairs[:, 2 * first : 2 * (first + window_width(n))].bitcast(U32)
            nc.vector.tensor_copy(dst.bitcast(U32), window.indirect(slot_offsets(s0, n)))

        def gather_early(a, h, s0, n):
            gather_pairs(early[a][:, h, 2 * s0 : 2 * (s0 + n)], a, h, s0, n)

        def gather_singles(e0, e1):
            for j in range(2):
                for e in range(e0, e1):
                    dst = early[1][:, 1, 2 * e * C : 2 * (e + 1) * C].rearrange("p (s j) -> p j s", j=2)
                    nc.scalar.activation(dst[:, j, :], singles[:, j, :].indirect(slot_offsets(e * C, C)), COPY)

        with tc.tile_pool(name="raw", bufs=1) as raw_pool:
            rows = xT.rearrange("(a p h j) t -> a h p j t", a=PASSES, p=P, h=2)
            scale_rows = w_scales.bitcast(I32).rearrange("e a (q r) c -> r q (e a) c", r=4)
            word_rows = w_words.bitcast(I32).rearrange("e a p c -> p (e a) c")
            w_view = w_sb[:].bitcast(I32).rearrange("p (m c) -> p m c", c=N // 2)
            raw = {}

            def load_tokens(a, h):
                raw[a, h] = raw_pool.tile([P, 2, T], F32, name="raw%d%d" % (a, h))
                nc.sync.dma_start(raw[a, h][:], rows[a, h])

            def load_scales(e0, e1):
                mats = slice(PASSES * e0, PASSES * e1)
                for r in range(4):
                    live = w_sc[r:P:32, :].bitcast(I32).rearrange("q (m c) -> q m c", c=N // 4)
                    nc.sync.dma_start(live[:, mats, :], scale_rows[r][:, mats, :])

            def load_words(e0, e1):
                mats = slice(PASSES * e0, PASSES * e1)
                nc.sync.dma_start(w_view[:, mats, :], word_rows[:, mats, :])

            load_tokens(0, 0)
            nc.sync.dma_start(offs_sb[:], offs)
            for a, h in LOAD_ORDER[1:]:
                load_tokens(a, h)
            load_scales(0, 8)
            load_words(0, 8)
            nc.sync.dma_start(bias[:], b)
            load_scales(8, 16)
            load_words(8, 16)
            load_scales(16, E + 1)
            load_words(16, E + 1)
            for r, pos in enumerate((pos1, pos2, pos3, pos4)):
                nc.sync.dma_start(pos_sb[r][:], pos)
            nc.sync.dma_start(gates[:], gate.rearrange("r n t -> n r t"))

            def cast(a, h):
                first = PLANE_SLOT[a, h] * T
                dst = pairs[:, 2 * first : 2 * (first + T)].rearrange("p (t j) -> p t j", j=2)
                src = raw[a, h][:].rearrange("p j t -> p t j")
                if (a, h) == LOAD_ORDER[0]:
                    nc.vector.tensor_copy(dst[:, :VECTOR_TOKENS, :], src[:, :VECTOR_TOKENS, :])
                    nc.scalar.copy(dst[:, VECTOR_TOKENS:, :], src[:, VECTOR_TOKENS:, :])
                elif (a, h) == LOAD_ORDER[1]:
                    nc.scalar.copy(dst, src)
                else:
                    nc.gpsimd.tensor_scalar(dst, src, 1.0, 0.0, MULT, ADD)

            cast(0, 0)
            gather_early(0, 0, 0, SLOTS // 2)
            gather_early(0, 0, SLOTS // 2, SLOTS // 2)
            cast(1, 0)
            nc.scalar.copy(singles[:], raw[1, 1][:])
            cast(1, 1)
            cast(0, 1)
            cast(2, 0)
            cast(2, 1)

        late = ctx.enter_context(tc.tile_pool(name="late", bufs=1))
        last_halves = {}
        grouped = {}
        shared = {}
        accs = {}

        def gather_last(c):
            last_halves[c] = ring.tile([P, 2, 2 * BANK], BF16, name="last_halves", align_bytes=64, bufs=2)
            for h in range(2):
                gather_pairs(last_halves[c][:, h, :], PASSES - 1, h, c * BANK, BANK)

        def interleave(a, s0, n):
            if a == PASSES - 1:
                src = last_halves[s0 // BANK][:].bitcast(U32)
            else:
                src = early[a][:].bitcast(U32)[:, :, s0 : s0 + n]
            grouped[a, s0] = ring.tile([P, 4 * n], BF16, name="grouped", align_bytes=64, bufs=3)
            nc.scalar.copy(
                grouped[a, s0][:].bitcast(U32).rearrange("p (s h) -> p s h", h=2), src.rearrange("p h s -> p s h")
            )

        def quantize_from(src, a, s0, n):
            nc.vector.quantize_mx(
                out=codes[:, a, s0 : s0 + n].bitcast(FP8X4), scales=scales[:, a, s0 : s0 + n], in_=src
            )

        def quantize(a, s0, n):
            quantize_from(grouped[a, s0][:], a, s0, n)

        def matmul(acc, e, a, s0, n):
            m = e * PASSES + a
            nc.tensor.matmul_mx(
                out=acc,
                lhsT=w_sb[:, m * 2 * N : (m + 1) * 2 * N].bitcast(FP4X4),
                lhsT_scale=w_sc[:, m * N : (m + 1) * N],
                rhs=codes[:, a, s0 : s0 + n].bitcast(FP8X4),
                rhs_scale=scales[:, a, s0 : s0 + n],
                start=(a == 0),
                stop=(a == PASSES - 1),
            )

        def open_own():
            for e in range(OWN_FIRST, E):
                own = psum.tile([P, C], F32, name="own%d" % e)
                accs[e] = own[:]
                for a in range(PASSES - 1):
                    matmul(accs[e], e, a, e * C, C)

        def multiply(c):
            if 4 * c >= OWN_FIRST:
                for e in range(4 * c, 4 * c + 4):
                    matmul(accs[e], e, PASSES - 1, e * C, C)
            else:
                acc = psum.tile([P, BANK], F32, name="acc", bufs=2)
                for j in range(4):
                    e = 4 * c + j
                    accs[e] = acc[:, j * C : (j + 1) * C]
                    for a in range(PASSES):
                        matmul(accs[e], e, a, e * C, C)

        def evacuate(c):
            for e in range(4 * c, 4 * c + 4):
                if e >= E - VECTOR_EXPERTS:
                    nc.vector.tensor_scalar_add(y[:, e * C : (e + 1) * C], accs[e], bias[:, e : e + 1])
                else:
                    nc.scalar.activation(y[:, e * C : (e + 1) * C], accs[e], IDENTITY, bias=bias[:, e : e + 1])

        planes = pairs[:, : 2 * PLANE_SLOTS * T].rearrange("p (g t j) -> p g t j", t=T, j=2)

        def group_shared(a):
            lo, hi = PLANE_SLOT[a, 0], PLANE_SLOT[a, 1]
            shared[a] = late.tile([P, 4 * T], BF16, name="shared%d" % a, align_bytes=64)
            nc.gpsimd.tensor_scalar(
                shared[a][:].rearrange("p (t h j) -> p t h j", h=2, j=2),
                planes[:, lo : hi + 1 : hi - lo, :, :].rearrange("p h t j -> p t h j"),
                1.0,
                0.0,
                MULT,
                ADD,
            )

        token_cuts = ((0, BANK), (BANK, T - BANK))

        def quantize_shared(a):
            for t0, n in token_cuts:
                quantize_from(shared[a][:, 4 * t0 : 4 * (t0 + n)], a, SHARED_AT[a] + t0, n)

        group_shared(0)
        group_shared(1)
        group_shared(2)
        gather_early(1, 0, 0, SLOTS // 2)
        gather_early(1, 0, SLOTS // 2, SLOTS // 2)
        gather_early(0, 1, 0, 1024)
        gather_early(0, 1, 1024, 1536)
        gather_singles(0, 14)
        interleave(0, 0, 1024)
        gather_singles(14, 16)
        interleave(0, 1024, 1024)
        gather_singles(16, 18)
        interleave(1, 0, 1024)
        gather_last(0)
        interleave(2, 0, BANK)
        gather_last(1)
        gather_singles(18, E)
        quantize(0, 0, 1024)
        quantize(0, 1024, 1024)
        interleave(0, 2048, BANK)
        quantize(0, 2048, BANK)
        gather_last(2)
        quantize(2, 0, BANK)
        interleave(2, 512, BANK)
        quantize(1, 0, 1024)
        interleave(1, 1024, 1024)
        quantize(1, 1024, 1024)
        multiply(0)
        evacuate(0)
        quantize(2, 512, BANK)
        gather_last(3)
        interleave(2, 1024, BANK)
        interleave(1, 2048, BANK)
        quantize(2, 1024, BANK)
        quantize(1, 2048, BANK)
        gather_last(4)
        multiply(1)
        open_own()
        interleave(2, 1536, BANK)
        quantize(2, 1536, BANK)
        interleave(2, 2048, BANK)
        evacuate(1)
        multiply(2)
        quantize_shared(0)
        evacuate(2)
        quantize(2, 2048, BANK)
        multiply(3)
        evacuate(3)
        quantize_shared(1)
        quantize_shared(2)
        multiply(4)
        evacuate(4)
        for t0, n in token_cuts:
            acc = psum.tile([P, n], F32, name="shared_acc%d" % t0)
            for a in range(PASSES):
                matmul(acc[:], E, a, SHARED_AT[a] + t0, n)
            nc.scalar.activation(ys[:, t0 : t0 + n], acc[:], IDENTITY, bias=bias[:, E : E + 1])

        terms = [late.tile([P, T], F32, name="term%d" % r) for r in range(TOP)]

        def fetch(r):
            nc.vector.tensor_tensor(terms[r][:], y[:].indirect(pos_sb[r][:]), gates[:, r, :], MULT)

        blocks = T // P
        turned = [psum.tile([P, P], F32, name="own%d" % (OWN_FIRST + i)) for i in range(blocks - 1)]
        turned.append(psum.tile([P, P], F32, name="acc", bufs=2))

        def add_turned(src, start, stop):
            for i in range(blocks):
                nc.tensor.matmul(
                    turned[i][:], src[:, i * P : (i + 1) * P], ident[:], start=start, stop=stop, is_transpose=True
                )

        add_turned(ys, True, False)
        fetch(0)
        add_turned(terms[0], False, False)
        fetch(1)
        add_turned(terms[1], False, True)
        fetch(2)
        fetch(3)
        partial = late.tile([P, blocks, P], F32)
        split = 3 * P
        back = [psum.tile([P, split], F32, name="acc", bufs=2), psum.tile([P, T - split], F32, name="shared_acc0")]
        for i in range(blocks):
            nc.scalar.copy(partial[:, i, :], turned[i][:])
            col = i * P % split
            nc.tensor.transpose(back[i * P // split][:, col : col + P], partial[:, i, :], ident[:])
        cuts = (slice(0, split), slice(split, T))
        for half, cols in enumerate(cuts):
            nc.vector.tensor_tensor(terms[2][:, cols], back[half][:], terms[2][:, cols], ADD)
        for cols in cuts:
            nc.vector.tensor_tensor(terms[2][:, cols], terms[2][:, cols], terms[3][:, cols], ADD)
            nc.sync.dma_start(out[:, cols], terms[2][:, cols])
